import numpy as np, ml_dtypes
CORES = [16,23,24,31,64,71]
N = 6
F = 128
GROUPS = [[0,1],[2,3],[4,5]]
def setup_inputs(rng):
    return {"x": rng.standard_normal((N, 128, F), dtype=np.float32).astype(ml_dtypes.bfloat16), "w": (rng.standard_normal((N, 128, 128), dtype=np.float32) / 11).astype(ml_dtypes.bfloat16)}
def setup_inputs_big(rng):
    d = setup_inputs(rng)
    for k in ("x", "w"): d[k] = (d[k].astype(np.float32) * 1024.0).astype(d[k].dtype)
    return d
def setup_inputs_small(rng):
    d = setup_inputs(rng)
    for k in ("x", "w"): d[k] = (d[k].astype(np.float32) * (1 / 1024.0)).astype(d[k].dtype)
    return d
def setup_inputs_apart(rng):
    d = setup_inputs(rng)
    f = (10.0 ** rng.permutation(np.linspace(-1.5, 1.5, N))).astype(np.float32).reshape(N, 1, 1)
    for k in ("x", "w"): d[k] = (d[k].astype(np.float32) * f).astype(d[k].dtype)
    return d
def reference(x, w):
    X, W = x.astype(np.float64), w.astype(np.float64)
    s = sum(W[g[0]].T @ np.maximum(sum(X[j] for j in g), 0.0) for g in GROUPS).astype(ml_dtypes.bfloat16)
    return {"y": np.broadcast_to(s, (N,) + s.shape)}

@@ -1,0 +1,139 @@
+from concourse.bass import DstId, RemoteDMATransfer
+from concourse.mybir import AluOpType
+
+F = 128
+K_IN = 8
+K_OUT = 8
+
+SCRATCH = {
+    "own": ("sbuf", [128, 2 * F], "bfloat16"),
+    "peer": ("sbuf", [128, 2 * F], "bfloat16"),
+    "zero": ("sbuf", [128, F], "bfloat16"),
+    "m": ("sbuf", [128, F], "bfloat16"),
+    "pb": ("sbuf", [128, F], "bfloat16"),
+    "rin": ("sbuf", [128, 3 * F], "bfloat16"),
+    "yb": ("sbuf", [128, F], "bfloat16"),
+    "neg": ("psum", [128, 512], "float32"),
+    "pp": ("psum", [128, 512], "float32"),
+    "acc": ("psum", [128, 512], "float32"),
+}
+SEMAPHORES = ["ldx", "ldw", "zs", "ns", "xin", "ms", "mm", "pc", "sent", "p0", "p1", "p2", "a1", "ys", "st"]
+
+
+def _engines(mask, k):
+    out, n, b = 0, 0, 0
+    while n < k:
+        if (mask >> b) & 1:
+            out |= 1 << b
+            n += 1
+        b += 1
+    return out
+
+
+def _hops(topo, s, d):
+    cs, cd = topo.chip(s), topo.chip(d)
+    if cs == cd:
+        return 0
+    return 1 if (topo.mates(cs, cd) or topo.same_plane(cs, cd)) else 2
+
+
+def _plan(T, topo):
+    cores = list(T.cores)
+    send, src = {}, {}
+    for gi, mem in enumerate(T.tables["GROUPS"]):
+        mc = [cores[r] for r in mem]
+        for s in mc:
+            send[s] = []
+        dests = [c for c in cores if c not in mc]
+        dests.sort(key=lambda d: sum(1 for s in mc if topo.may_write(s, d)))
+        for d in dests:
+            s = min([s for s in mc if topo.may_write(s, d)], key=lambda c: len(send[c]))
+            send[s].append(d)
+            src[(gi, d)] = s
+    return send, src
+
+
+def rank_program(g, core, T, topo):
+    rank = T.rank_of(core)
+    if rank is None:
+        return
+    groups = T.tables["GROUPS"]
+    cores = list(T.cores)
+    gi = [i for i, mem in enumerate(groups) if rank in mem][0]
+    first = groups[gi][0] == rank
+    peer = [cores[r] for r in groups[gi] if r != rank][0]
+    send, src = _plan(T, topo)
+    S = T.sem
+
+    x_own, w_own = T.own[:, 0:F], T.own[:, F:2 * F]
+    x_peer = T.peer[:, 0:F]
+    w_g = w_own if first else T.peer[:, F:2 * F]
+    pp, neg, acc = T.pp[:, 0:F], T.neg[:, 0:F], T.acc[:, 0:F]
+
+    m_all = topo.mask(core, peer)
+    for d in cores:
+        if d != core:
+            m_all &= topo.mask(core, d)
+    m_in = _engines(m_all, K_IN)
+    m_out = _engines(m_all, K_OUT)
+
+    g.sync.dma_start(x_own, T.x[:, :]).then_inc(S.ldx, 16)
+    if first:
+        g.scalar.dma_start(w_own, T.w[:, :]).then_inc(S.ldw, 16)
+
+    rid, pid, _ = topo.addr(peer)
+    g.wait_ge(S.ldx, 16)
+    if first:
+        g.wait_ge(S.ldw, 16)
+        g.remote_dma(T.peer[:, :], T.own[:, :], S.xin, S.sent, pid, rid, m_in)
+    else:
+        g.remote_dma(x_peer, x_own, S.xin, S.sent, pid, rid, m_in)
+    n_sent = K_IN
+
+    v, t = g.vector, g.tensor
+    v.memset(T.zero[:, :], 0.0).then_inc(S.zs, 1)
+    v.wait_ge(S.zs, 1)
+    v.wait_ge(S.ldx, 16)
+    v.tensor_tensor(neg, T.zero[:, :], x_own, AluOpType.subtract).then_inc(S.ns, 1)
+    v.wait_ge(S.ns, 1)
+    v.wait_ge(S.xin, K_IN)
+    v.tensor_tensor(T.m[:, :], x_peer, neg, AluOpType.max).then_inc(S.ms, 1)
+
+    t.wait_ge(S.ldx, 16)
+    if first:
+        t.wait_ge(S.ldw, 16)
+    else:
+        t.wait_ge(S.xin, K_IN)
+    t.matmul(pp, w_g, x_own, start=True, stop=False)
+    t.wait_ge(S.ms, 1)
+    t.matmul(pp, w_g, T.m[:, :], start=False, stop=True).then_inc(S.mm, 1)
+
+    v.wait_ge(S.mm, 1)
+    if send[core]:
+        v.tensor_copy(T.pb[:, :], pp).then_inc(S.pc, 1)
+
+        g.wait_ge(S.pc, 1)
+        slot = T.rin[:, gi * F:(gi + 1) * F]
+        ids = []
+        for d in send[core]:
+            r, p, _ = topo.addr(d)
+            ids.append(DstId(rid=r, pnc=p))
+        g.remote_dma_fused(
+            [RemoteDMATransfer(dst_ids=ids, dma_engine_mask=m_out, remote_sem=S["p%d" % gi],
+                               src=T.pb[:, :], dsts=[slot for _ in ids], alu_op=0)],
+            local_sem=S.sent)
+        n_sent += K_OUT
+
+    others = [k for k in range(len(groups)) if k != gi]
+    others.sort(key=lambda k: (len(send[src[(k, core)]]), _hops(topo, src[(k, core)], core)))
+    e, l = others
+    v.wait_ge(S["p%d" % e], K_OUT)
+    v.tensor_tensor(acc, pp, T.rin[:, e * F:(e + 1) * F], AluOpType.add).then_inc(S.a1, 1)
+    v.wait_ge(S.a1, 1)
+    v.wait_ge(S["p%d" % l], K_OUT)
+    v.tensor_tensor(T.yb[:, :], acc, T.rin[:, l * F:(l + 1) * F], AluOpType.add).then_inc(S.ys, 1)
+
+    g.sync.wait_ge(S.ys, 1)
+    g.sync.dma_start(T.y[:, :], T.yb[:, :]).then_inc(S.st, 16)
+    g.sync.wait_ge(S.st, 16)
+    g.wait_ge(S.sent, n_sent)

@@ -2,8 +2,7 @@ from concourse.bass import DstId, RemoteDMATransfer
 from concourse.mybir import AluOpType
 
 F = 128
-K_IN = 8
-K_OUT = 8
+K = 8
 
 SCRATCH = {
     "own": ("sbuf", [128, 2 * F], "bfloat16"),
@@ -14,10 +13,13 @@ SCRATCH = {
     "rin": ("sbuf", [128, 3 * F], "bfloat16"),
     "yb": ("sbuf", [128, F], "bfloat16"),
     "neg": ("psum", [128, 512], "float32"),
+    "ph0": ("psum", [128, 512], "float32"),
+    "ph1": ("psum", [128, 512], "float32"),
     "pp": ("psum", [128, 512], "float32"),
     "acc": ("psum", [128, 512], "float32"),
 }
-SEMAPHORES = ["ldx", "ldw", "zs", "ns", "xin", "ms", "mm", "pc", "sent", "p0", "p1", "p2", "a1", "ys", "st"]
+SEMAPHORES = ["ldx", "ldw", "xown", "zs", "ns", "xin", "ms0", "ms1", "mm0", "mm1", "mm", "pc", "sent",
+              "p0", "p1", "p2", "a1", "ys", "st"]
 
 
 def _engines(mask, k):
@@ -39,7 +41,7 @@ def _hops(topo, s, d):
 
 def _plan(T, topo):
     cores = list(T.cores)
-    send, src = {}, {}
+    send, src, helper = {}, {}, {}
     for gi, mem in enumerate(T.tables["GROUPS"]):
         mc = [cores[r] for r in mem]
         for s in mc:
@@ -49,91 +51,149 @@ def _plan(T, topo):
         for d in dests:
             s = min([s for s in mc if topo.may_write(s, d)], key=lambda c: len(send[c]))
             send[s].append(d)
-            src[(gi, d)] = s
-    return send, src
+        helper[gi] = None
+        busy = max(mc, key=lambda c: len(send[c]))
+        if min(len(send[c]) for c in mc) == 0:
+            near = sorted(send[busy], key=lambda d: _hops(topo, busy, d))
+            moved = near[:len(near) // 2]
+            cand = [c for c in range(max(cores) + 1)
+                    if c not in cores and topo.chip(c) == topo.chip(busy) and topo.die(c) != topo.die(busy)
+                    and all(topo.may_write(c, d) for d in moved)]
+            if cand:
+                helper[gi] = cand[0]
+                send[cand[0]] = moved
+                send[busy] = [d for d in send[busy] if d not in moved]
+        for s in mc + [helper[gi]]:
+            for d in send.get(s, []):
+                src[(gi, d)] = s
+    return send, src, helper
 
 
 def rank_program(g, core, T, topo):
-    rank = T.rank_of(core)
-    if rank is None:
-        return
     groups = T.tables["GROUPS"]
     cores = list(T.cores)
-    gi = [i for i, mem in enumerate(groups) if rank in mem][0]
-    first = groups[gi][0] == rank
-    peer = [cores[r] for r in groups[gi] if r != rank][0]
-    send, src = _plan(T, topo)
+    send, src, helper = _plan(T, topo)
+    rank = T.rank_of(core)
+    if rank is None:
+        mine = [i for i in helper if helper[i] == core]
+        if not mine:
+            return
+        gi, role = mine[0], "h"
+    else:
+        gi = [i for i, mem in enumerate(groups) if rank in mem][0]
+        role = "a" if groups[gi][0] == rank else "b"
+    a_core, b_core = cores[groups[gi][0]], cores[groups[gi][1]]
+    h_core = helper[gi]
     S = T.sem
 
     x_own, w_own = T.own[:, 0:F], T.own[:, F:2 * F]
     x_peer = T.peer[:, 0:F]
-    w_g = w_own if first else T.peer[:, F:2 * F]
+    w_g = w_own if role == "a" else T.peer[:, F:2 * F]
     pp, neg, acc = T.pp[:, 0:F], T.neg[:, 0:F], T.acc[:, 0:F]
 
-    m_all = topo.mask(core, peer)
+    on_chip = topo.mask(core, a_core if core != a_core else b_core)
+    m_all = on_chip
     for d in cores:
         if d != core:
             m_all &= topo.mask(core, d)
-    m_in = _engines(m_all, K_IN)
-    m_out = _engines(m_all, K_OUT)
+    m_k = _engines(m_all, K)
+    m_more = _engines(on_chip & ~m_k, K)
+    n_sent = 0
 
-    g.sync.dma_start(x_own, T.x[:, :]).then_inc(S.ldx, 16)
-    if first:
+    def dst_id(c):
+        r, p, _ = topo.addr(c)
+        return DstId(rid=r, pnc=p)
+
+    if role == "a":
+        g.sync.dma_start(x_own, T.x[:, :]).then_inc(S.ldx, 16)
         g.scalar.dma_start(w_own, T.w[:, :]).then_inc(S.ldw, 16)
-
-    rid, pid, _ = topo.addr(peer)
-    g.wait_ge(S.ldx, 16)
-    if first:
+        xs, xv = S.ldx, 16
+        g.wait_ge(S.ldx, 16)
         g.wait_ge(S.ldw, 16)
-        g.remote_dma(T.peer[:, :], T.own[:, :], S.xin, S.sent, pid, rid, m_in)
+        tr = [RemoteDMATransfer(dst_ids=[dst_id(b_core)], dma_engine_mask=m_k, remote_sem=S.xin,
+                                src=T.own[:, :], dst=T.peer[:, :], alu_op=0)]
+        n_sent += K
+        if h_core is not None:
+            tr.append(RemoteDMATransfer(dst_ids=[dst_id(h_core)], dma_engine_mask=m_more, remote_sem=S.xin,
+                                        src=T.own[:, :], dst=T.peer[:, :], alu_op=0))
+            n_sent += K
+        g.remote_dma_fused(tr, local_sem=S.sent)
+    elif role == "b":
+        g.sync.dma_start(x_own, T.x[:, :]).then_inc(S.ldx, 16)
+        xs, xv = S.ldx, 16
+        g.wait_ge(S.ldx, 16)
+        if h_core is None:
+            rid, pid, _ = topo.addr(a_core)
+            g.remote_dma(x_peer, x_own, S.xin, S.sent, pid, rid, m_k)
+        else:
+            rid, pid, _ = topo.addr(h_core)
+            g.remote_dma(x_own, x_own, S.xown, S.sent, pid, rid, m_k)
+        n_sent += K
     else:
-        g.remote_dma(x_peer, x_own, S.xin, S.sent, pid, rid, m_in)
-    n_sent = K_IN
+        xs, xv = S.xown, K
+        rid, pid, _ = topo.addr(a_core)
+        g.wait_ge(S.xown, K)
+        g.remote_dma(x_peer, x_own, S.xin, S.sent, pid, rid, m_k)
+        n_sent += K
 
     v, t = g.vector, g.tensor
+    H = F // 2
+    parts = [(0, H), (H, F)] if send[core] else [(0, F)]
+    banks = [T.ph0[:, 0:H], T.ph1[:, 0:H]]
+
     v.memset(T.zero[:, :], 0.0).then_inc(S.zs, 1)
     v.wait_ge(S.zs, 1)
-    v.wait_ge(S.ldx, 16)
+    v.wait_ge(xs, xv)
     v.tensor_tensor(neg, T.zero[:, :], x_own, AluOpType.subtract).then_inc(S.ns, 1)
     v.wait_ge(S.ns, 1)
-    v.wait_ge(S.xin, K_IN)
-    v.tensor_tensor(T.m[:, :], x_peer, neg, AluOpType.max).then_inc(S.ms, 1)
+    v.wait_ge(S.xin, K)
+    for i, (lo, hi) in enumerate(parts):
+        v.tensor_tensor(T.m[:, lo:hi], T.peer[:, lo:hi], T.neg[:, lo:hi], AluOpType.max).then_inc(S["ms%d" % i], 1)
 
-    t.wait_ge(S.ldx, 16)
-    if first:
+    t.wait_ge(xs, xv)
+    if role == "a":
         t.wait_ge(S.ldw, 16)
     else:
-        t.wait_ge(S.xin, K_IN)
-    t.matmul(pp, w_g, x_own, start=True, stop=False)
-    t.wait_ge(S.ms, 1)
-    t.matmul(pp, w_g, T.m[:, :], start=False, stop=True).then_inc(S.mm, 1)
-
-    v.wait_ge(S.mm, 1)
+        t.wait_ge(S.xin, K)
     if send[core]:
-        v.tensor_copy(T.pb[:, :], pp).then_inc(S.pc, 1)
+        for i, (lo, hi) in enumerate(parts):
+            t.matmul(banks[i], w_g, T.own[:, lo:hi], start=True, stop=False)
+    if role != "h":
+        t.matmul(pp, w_g, x_own, start=True, stop=False)
+    for i, (lo, hi) in enumerate(parts):
+        t.wait_ge(S["ms%d" % i], 1)
+        if send[core]:
+            t.matmul(banks[i], w_g, T.m[:, lo:hi], start=False, stop=True).then_inc(S["mm%d" % i], 1)
+    if role != "h":
+        t.matmul(pp, w_g, T.m[:, :], start=False, stop=True).then_inc(S.mm, 1)
 
-        g.wait_ge(S.pc, 1)
+    if send[core]:
+        for i, (lo, hi) in enumerate(parts):
+            v.wait_ge(S["mm%d" % i], 1)
+            v.tensor_copy(T.pb[:, lo:hi], banks[i]).then_inc(S.pc, 1)
+
+        g.wait_ge(S.pc, len(parts))
         slot = T.rin[:, gi * F:(gi + 1) * F]
-        ids = []
-        for d in send[core]:
-            r, p, _ = topo.addr(d)
-            ids.append(DstId(rid=r, pnc=p))
         g.remote_dma_fused(
-            [RemoteDMATransfer(dst_ids=ids, dma_engine_mask=m_out, remote_sem=S["p%d" % gi],
-                               src=T.pb[:, :], dsts=[slot for _ in ids], alu_op=0)],
+            [RemoteDMATransfer(dst_ids=[dst_id(d) for d in send[core]], dma_engine_mask=m_k,
+                               remote_sem=S["p%d" % gi], src=T.pb[:, :], dsts=[slot for _ in send[core]], alu_op=0)],
             local_sem=S.sent)
-        n_sent += K_OUT
+        n_sent += K
 
-    others = [k for k in range(len(groups)) if k != gi]
-    others.sort(key=lambda k: (len(send[src[(k, core)]]), _hops(topo, src[(k, core)], core)))
-    e, l = others
-    v.wait_ge(S["p%d" % e], K_OUT)
-    v.tensor_tensor(acc, pp, T.rin[:, e * F:(e + 1) * F], AluOpType.add).then_inc(S.a1, 1)
-    v.wait_ge(S.a1, 1)
-    v.wait_ge(S["p%d" % l], K_OUT)
-    v.tensor_tensor(T.yb[:, :], acc, T.rin[:, l * F:(l + 1) * F], AluOpType.add).then_inc(S.ys, 1)
+    if role != "h":
+        def lateness(k):
+            s = src[(k, core)]
+            kind = 0 if s == cores[groups[k][0]] else (1 if s in cores else 2)
+            return (kind, _hops(topo, s, core))
+        e, l = sorted([k for k in range(len(groups)) if k != gi], key=lateness)
+        v.wait_ge(S.mm, 1)
+        v.wait_ge(S["p%d" % e], K)
+        v.tensor_tensor(acc, pp, T.rin[:, e * F:(e + 1) * F], AluOpType.add).then_inc(S.a1, 1)
+        v.wait_ge(S.a1, 1)
+        v.wait_ge(S["p%d" % l], K)
+        v.tensor_tensor(T.yb[:, :], acc, T.rin[:, l * F:(l + 1) * F], AluOpType.add).then_inc(S.ys, 1)
 
-    g.sync.wait_ge(S.ys, 1)
-    g.sync.dma_start(T.y[:, :], T.yb[:, :]).then_inc(S.st, 16)
-    g.sync.wait_ge(S.st, 16)
+        g.sync.wait_ge(S.ys, 1)
+        g.sync.dma_start(T.y[:, :], T.yb[:, :]).then_inc(S.st, 16)
+        g.sync.wait_ge(S.st, 16)
     g.wait_ge(S.sent, n_sent)

from concourse.bass import DstId, RemoteDMATransfer
from concourse.mybir import AluOpType

F = 128
K = 8

SCRATCH = {
    "own": ("sbuf", [128, 2 * F], "bfloat16"),
    "peer": ("sbuf", [128, 2 * F], "bfloat16"),
    "zero": ("sbuf", [128, F], "bfloat16"),
    "m": ("sbuf", [128, F], "bfloat16"),
    "pb": ("sbuf", [128, F], "bfloat16"),
    "rin": ("sbuf", [128, 3 * F], "bfloat16"),
    "yb": ("sbuf", [128, F], "bfloat16"),
    "neg": ("psum", [128, 512], "float32"),
    "ph0": ("psum", [128, 512], "float32"),
    "ph1": ("psum", [128, 512], "float32"),
    "pp": ("psum", [128, 512], "float32"),
    "acc": ("psum", [128, 512], "float32"),
}
SEMAPHORES = ["ldx", "ldw", "xown", "zs", "ns", "xin", "ms0", "ms1", "mm0", "mm1", "mm", "pc", "sent",
              "p0", "p1", "p2", "a1", "ys", "st"]


def _engines(mask, k):
    out, n, b = 0, 0, 0
    while n < k:
        if (mask >> b) & 1:
            out |= 1 << b
            n += 1
        b += 1
    return out


def _hops(topo, s, d):
    cs, cd = topo.chip(s), topo.chip(d)
    if cs == cd:
        return 0
    return 1 if (topo.mates(cs, cd) or topo.same_plane(cs, cd)) else 2


def _plan(T, topo):
    cores = list(T.cores)
    send, src, helper = {}, {}, {}
    for gi, mem in enumerate(T.tables["GROUPS"]):
        mc = [cores[r] for r in mem]
        for s in mc:
            send[s] = []
        dests = [c for c in cores if c not in mc]
        dests.sort(key=lambda d: sum(1 for s in mc if topo.may_write(s, d)))
        for d in dests:
            s = min([s for s in mc if topo.may_write(s, d)], key=lambda c: len(send[c]))
            send[s].append(d)
        helper[gi] = None
        busy = max(mc, key=lambda c: len(send[c]))
        if min(len(send[c]) for c in mc) == 0:
            near = sorted(send[busy], key=lambda d: _hops(topo, busy, d))
            moved = near[:len(near) // 2]
            cand = [c for c in range(max(cores) + 1)
                    if c not in cores and topo.chip(c) == topo.chip(busy) and topo.die(c) != topo.die(busy)
                    and all(topo.may_write(c, d) for d in moved)]
            if cand:
                helper[gi] = cand[0]
                send[cand[0]] = moved
                send[busy] = [d for d in send[busy] if d not in moved]
        for s in mc + [helper[gi]]:
            for d in send.get(s, []):
                src[(gi, d)] = s
    return send, src, helper


def rank_program(g, core, T, topo):
    groups = T.tables["GROUPS"]
    cores = list(T.cores)
    send, src, helper = _plan(T, topo)
    rank = T.rank_of(core)
    if rank is None:
        mine = [i for i in helper if helper[i] == core]
        if not mine:
            return
        gi, role = mine[0], "h"
    else:
        gi = [i for i, mem in enumerate(groups) if rank in mem][0]
        role = "a" if groups[gi][0] == rank else "b"
    a_core, b_core = cores[groups[gi][0]], cores[groups[gi][1]]
    h_core = helper[gi]
    S = T.sem

    x_own, w_own = T.own[:, 0:F], T.own[:, F:2 * F]
    x_peer = T.peer[:, 0:F]
    w_g = w_own if role == "a" else T.peer[:, F:2 * F]
    pp, neg, acc = T.pp[:, 0:F], T.neg[:, 0:F], T.acc[:, 0:F]

    on_chip = topo.mask(core, a_core if core != a_core else b_core)
    m_all = on_chip
    for d in cores:
        if d != core:
            m_all &= topo.mask(core, d)
    m_k = _engines(m_all, K)
    m_more = _engines(on_chip & ~m_k, K)
    n_sent = 0

    def dst_id(c):
        r, p, _ = topo.addr(c)
        return DstId(rid=r, pnc=p)

    if role == "a":
        g.sync.dma_start(x_own, T.x[:, :]).then_inc(S.ldx, 16)
        g.scalar.dma_start(w_own, T.w[:, :]).then_inc(S.ldw, 16)
        xs, xv = S.ldx, 16
        g.wait_ge(S.ldx, 16)
        g.wait_ge(S.ldw, 16)
        tr = [RemoteDMATransfer(dst_ids=[dst_id(b_core)], dma_engine_mask=m_k, remote_sem=S.xin,
                                src=T.own[:, :], dst=T.peer[:, :], alu_op=0)]
        n_sent += K
        if h_core is not None:
            tr.append(RemoteDMATransfer(dst_ids=[dst_id(h_core)], dma_engine_mask=m_more, remote_sem=S.xin,
                                        src=T.own[:, :], dst=T.peer[:, :], alu_op=0))
            n_sent += K
        g.remote_dma_fused(tr, local_sem=S.sent)
    elif role == "b":
        g.sync.dma_start(x_own, T.x[:, :]).then_inc(S.ldx, 16)
        xs, xv = S.ldx, 16
        g.wait_ge(S.ldx, 16)
        if h_core is None:
            rid, pid, _ = topo.addr(a_core)
            g.remote_dma(x_peer, x_own, S.xin, S.sent, pid, rid, m_k)
        else:
            rid, pid, _ = topo.addr(h_core)
            g.remote_dma(x_own, x_own, S.xown, S.sent, pid, rid, m_k)
        n_sent += K
    else:
        xs, xv = S.xown, K
        rid, pid, _ = topo.addr(a_core)
        g.wait_ge(S.xown, K)
        g.remote_dma(x_peer, x_own, S.xin, S.sent, pid, rid, m_k)
        n_sent += K

    v, t = g.vector, g.tensor
    H = F // 2
    parts = [(0, H), (H, F)] if send[core] else [(0, F)]
    banks = [T.ph0[:, 0:H], T.ph1[:, 0:H]]

    v.memset(T.zero[:, :], 0.0).then_inc(S.zs, 1)
    v.wait_ge(S.zs, 1)
    v.wait_ge(xs, xv)
    v.tensor_tensor(neg, T.zero[:, :], x_own, AluOpType.subtract).then_inc(S.ns, 1)
    v.wait_ge(S.ns, 1)
    v.wait_ge(S.xin, K)
    for i, (lo, hi) in enumerate(parts):
        v.tensor_tensor(T.m[:, lo:hi], T.peer[:, lo:hi], T.neg[:, lo:hi], AluOpType.max).then_inc(S["ms%d" % i], 1)

    t.wait_ge(xs, xv)
    if role == "a":
        t.wait_ge(S.ldw, 16)
    else:
        t.wait_ge(S.xin, K)
    if send[core]:
        for i, (lo, hi) in enumerate(parts):
            t.matmul(banks[i], w_g, T.own[:, lo:hi], start=True, stop=False)
    if role != "h":
        t.matmul(pp, w_g, x_own, start=True, stop=False)
    for i, (lo, hi) in enumerate(parts):
        t.wait_ge(S["ms%d" % i], 1)
        if send[core]:
            t.matmul(banks[i], w_g, T.m[:, lo:hi], start=False, stop=True).then_inc(S["mm%d" % i], 1)
    if role != "h":
        t.matmul(pp, w_g, T.m[:, :], start=False, stop=True).then_inc(S.mm, 1)

    if send[core]:
        for i, (lo, hi) in enumerate(parts):
            v.wait_ge(S["mm%d" % i], 1)
            v.tensor_copy(T.pb[:, lo:hi], banks[i]).then_inc(S.pc, 1)

        g.wait_ge(S.pc, len(parts))
        slot = T.rin[:, gi * F:(gi + 1) * F]
        g.remote_dma_fused(
            [RemoteDMATransfer(dst_ids=[dst_id(d) for d in send[core]], dma_engine_mask=m_k,
                               remote_sem=S["p%d" % gi], src=T.pb[:, :], dsts=[slot for _ in send[core]], alu_op=0)],
            local_sem=S.sent)
        n_sent += K

    if role != "h":
        def lateness(k):
            s = src[(k, core)]
            kind = 0 if s == cores[groups[k][0]] else (1 if s in cores else 2)
            return (kind, _hops(topo, s, core))
        e, l = sorted([k for k in range(len(groups)) if k != gi], key=lateness)
        v.wait_ge(S.mm, 1)
        v.wait_ge(S["p%d" % e], K)
        v.tensor_tensor(acc, pp, T.rin[:, e * F:(e + 1) * F], AluOpType.add).then_inc(S.a1, 1)
        v.wait_ge(S.a1, 1)
        v.wait_ge(S["p%d" % l], K)
        v.tensor_tensor(T.yb[:, :], acc, T.rin[:, l * F:(l + 1) * F], AluOpType.add).then_inc(S.ys, 1)

        g.sync.wait_ge(S.ys, 1)
        g.sync.dma_start(T.y[:, :], T.yb[:, :]).then_inc(S.st, 16)
        g.sync.wait_ge(S.st, 16)
    g.wait_ge(S.sent, n_sent)
